import numpy as np, ml_dtypes
CORES = [24,40,56,80,88,96]
N = 6
NP, NBK, TK, CAP = 3, 4, 128, 4
DEST = [[3,4,4,5],[5,3,5,3],[4,5,3,4]]
def setup_inputs(rng):
    return {"x": rng.standard_normal((N, 128, NBK * TK), dtype=np.float32).astype(ml_dtypes.bfloat16), "w": (rng.standard_normal((N, 128, 128), dtype=np.float32) / 8).astype(ml_dtypes.bfloat16)}
def setup_inputs_big(rng):
    d = setup_inputs(rng)
    for k in ("x", "w"): d[k] = (d[k].astype(np.float32) * 1024.0).astype(d[k].dtype)
    return d
def setup_inputs_small(rng):
    d = setup_inputs(rng)
    for k in ("x", "w"): d[k] = (d[k].astype(np.float32) * (1 / 1024.0)).astype(d[k].dtype)
    return d
def setup_inputs_apart(rng):
    d = setup_inputs(rng)
    f = (10.0 ** rng.permutation(np.linspace(-1.5, 1.5, N))).astype(np.float32).reshape(N, 1, 1)
    for k in ("x", "w"): d[k] = (d[k].astype(np.float32) * f).astype(d[k].dtype)
    return d
def reference(x, w):
    X, W = x.astype(np.float64), w.astype(np.float64)
    y = np.full((N, 128, CAP * TK), np.nan); n = [0] * N
    for p in range(NP):
        for c in range(NBK):
            q = DEST[p][c]
            y[q][:, TK * n[q]:TK * n[q] + TK] = W[q].T @ np.maximum(W[p].T @ X[p][:, TK * c:TK * c + TK], 0.0)
            n[q] += 1
    return {"y": y.astype(ml_dtypes.bfloat16 if x.dtype != np.float64 else np.float64)}

@@ -1,0 +1,174 @@
+from concourse.bass import DstId, RemoteDMATransfer
+from concourse.mybir import AluOpType
+
+TK = 128
+ON_CHIP = 8
+OFF_CHIP = 8
+
+SCRATCH = {
+    "ws": ("sbuf", [128, 128], "bfloat16"),
+    "xs": ("sbuf", [128, 512], "bfloat16"),
+    "zs": ("sbuf", [128, 512], "float32"),
+    "hs": ("sbuf", [128, 512], "bfloat16"),
+    "land": ("sbuf", [128, 512], "bfloat16"),
+    "ys": ("sbuf", [128, 512], "bfloat16"),
+    "ps0": ("psum", [128, 512], "float32"),
+    "ps1": ("psum", [128, 512], "float32"),
+    "ps2": ("psum", [128, 512], "float32"),
+}
+SEMAPHORES = ["ld", "zero", "mm0", "mm1", "mm2", "ev0", "ev1", "ev2", "relay", "arr0", "arr1", "arr2", "sent", "st"]
+
+
+def _bits(mask):
+    return [b for b in range(mask.bit_length()) if (mask >> b) & 1]
+
+
+def _mask(bits):
+    m = 0
+    for b in bits:
+        m |= 1 << b
+    return m
+
+
+def _pow2(n):
+    k = 1
+    while 2 * k <= n:
+        k *= 2
+    return k
+
+
+def _plan(T, topo):
+    dest, cores = T.tables["DEST"], list(T.cores)
+    routes, nslot = [], {}
+    for p in range(len(dest)):
+        byq = {}
+        for c, q in enumerate(dest[p]):
+            if q not in byq:
+                byq[q] = {"p": p, "q": q, "blocks": [], "slot": nslot.get(q, 0), "via": None}
+            byq[q]["blocks"].append(c)
+            nslot[q] = nslot.get(q, 0) + 1
+        routes.extend(byq[q] for q in sorted(byq))
+
+    out_load, in_load, used = {}, {}, set(cores)
+    for r in sorted(routes, key=lambda r: (-len(r["blocks"]), r["p"], r["q"])):
+        src, dst, n = cores[r["p"]], cores[r["q"]], len(r["blocks"])
+        if topo.may_write(src, dst):
+            continue
+        cands = [c for c in range(topo.CORES_PER_CHIP * topo.CHIPS)
+                 if topo.chip(c) == topo.chip(src) and c not in used and topo.may_write(c, dst)]
+        via = min(cands, key=lambda c: (max(out_load.get((topo.chip(src), topo.die(c)), 0),
+                                            in_load.get((topo.chip(dst), topo.die(c)), 0)),
+                                        topo.die(c) != topo.die(src), c))
+        d = topo.die(via)
+        out_load[(topo.chip(src), d)] = out_load.get((topo.chip(src), d), 0) + n
+        in_load[(topo.chip(dst), d)] = in_load.get((topo.chip(dst), d), 0) + n
+        used.add(via)
+        r["via"] = via
+        r["mask2"] = _mask(_bits(topo.mask(via, dst))[:OFF_CHIP])
+
+    calls = {}
+    for p in range(len(dest)):
+        mine = sorted((r for r in routes if r["p"] == p), key=lambda r: (r["via"] is None, len(r["blocks"]), r["q"]))
+        off, calls[p] = 0, []
+        for k, r in enumerate(mine):
+            r["k"], r["off"] = k, off
+            off += TK * len(r["blocks"])
+            r["hop"] = cores[r["q"]] if r["via"] is None else r["via"]
+            last = calls[p][-1] if calls[p] else None
+            if last and (last[0]["via"] is None) == (r["via"] is None) and len(last[0]["blocks"]) == len(r["blocks"]):
+                last.append(r)
+            else:
+                calls[p].append([r])
+        for call in calls[p]:
+            common = topo.mask(cores[p], call[0]["hop"])
+            for r in call:
+                common &= topo.mask(cores[p], r["hop"])
+            bits = _bits(common)
+            for j, r in enumerate(call):
+                cap = ON_CHIP if topo.chip(r["hop"]) == topo.chip(cores[p]) else OFF_CHIP
+                r["mask1"] = _mask(bits[j::len(call)][:min(cap, _pow2(len(bits) // len(call)))])
+    return routes, calls
+
+
+def _count(mask):
+    return len(_bits(mask))
+
+
+def _rank_p(g, core, T, topo, calls):
+    mine = [r for call in calls for r in call]
+    widest = TK * max(len(r["blocks"]) for r in mine)
+    g.sync.dma_start(T.ws[:, :], T.w[:, :]).then_inc(T.sem.ld, 16)
+    g.scalar.dma_start(T.xs[:, :], T.x[:, :]).then_inc(T.sem.ld, 16)
+    g.vector.memset(T.zs[:, 0:widest], 0.0).then_inc(T.sem.zero, 1)
+    g.vector.wait_ge(T.sem.zero, 1)
+    g.tensor.wait_ge(T.sem.ld, 32)
+    for r in mine:
+        ps, mm, ev = T["ps%d" % r["k"]], T.sem["mm%d" % r["k"]], T.sem["ev%d" % r["k"]]
+        runs = []
+        for c in r["blocks"]:
+            if runs and runs[-1][0] + runs[-1][1] == c:
+                runs[-1][1] += 1
+            else:
+                runs.append([c, 1])
+        col = 0
+        for c0, n in runs:
+            g.tensor.matmul(ps[:, col:col + n * TK], T.ws[:, :], T.xs[:, c0 * TK:(c0 + n) * TK], True, True).then_inc(mm, 1)
+            col += n * TK
+        g.vector.wait_ge(mm, len(runs))
+        g.vector.tensor_tensor(T.hs[:, r["off"]:r["off"] + col], ps[:, 0:col], T.zs[:, 0:col], AluOpType.max).then_inc(ev, 1)
+    left = 0
+    for call in calls:
+        transfers = []
+        for r in call:
+            g.wait_ge(T.sem["ev%d" % r["k"]], 1)
+            n = TK * len(r["blocks"])
+            rid, pid, _ = topo.addr(r["hop"])
+            if r["via"] is None:
+                out, sem = T.land[:, TK * r["slot"]:TK * r["slot"] + n], T.sem["arr%d" % r["p"]]
+            else:
+                out, sem = T.hs[:, 0:n], T.sem.relay
+            transfers.append(RemoteDMATransfer(dst_ids=[DstId(rid=rid, pnc=pid)], dma_engine_mask=r["mask1"],
+                                               remote_sem=sem, src=T.hs[:, r["off"]:r["off"] + n], dst=out))
+            left += _count(r["mask1"])
+        g.remote_dma_fused(transfers, local_sem=T.sem.sent)
+    g.wait_ge(T.sem.sent, left)
+
+
+def _helper(g, core, T, topo, r):
+    n = TK * len(r["blocks"])
+    rid, pid, _ = topo.addr(T.cores[r["q"]])
+    g.wait_ge(T.sem.relay, _count(r["mask1"]))
+    g.remote_dma(out_ap=T.land[:, TK * r["slot"]:TK * r["slot"] + n], in_ap=T.hs[:, 0:n],
+                 remote_sem=T.sem["arr%d" % r["p"]], local_sem=T.sem.sent, pid=pid, routing_id=rid,
+                 dma_engine_mask=r["mask2"])
+    g.wait_ge(T.sem.sent, _count(r["mask2"]))
+
+
+def _rank_q(g, core, T, topo, mine):
+    g.sync.dma_start(T.ws[:, :], T.w[:, :]).then_inc(T.sem.ld, 16)
+    g.tensor.wait_ge(T.sem.ld, 16)
+    mine = sorted(mine, key=lambda r: (len(r["blocks"]), r["p"]))
+    queues = [g.scalar, g.sync]
+    for k, r in enumerate(mine):
+        a, n = TK * r["slot"], TK * len(r["blocks"])
+        ps, mm, ev, dq = T["ps%d" % k], T.sem["mm%d" % k], T.sem["ev%d" % k], queues[k % 2]
+        g.tensor.wait_ge(T.sem["arr%d" % r["p"]], _count(r["mask1"] if r["via"] is None else r["mask2"]))
+        g.tensor.matmul(ps[:, 0:n], T.ws[:, :], T.land[:, a:a + n], True, True).then_inc(mm, 1)
+        g.vector.wait_ge(mm, 1)
+        g.vector.tensor_copy(T.ys[:, a:a + n], ps[:, 0:n]).then_inc(ev, 1)
+        dq.wait_ge(ev, 1)
+        dq.dma_start(T.y[:, a:a + n], T.ys[:, a:a + n]).then_inc(T.sem.st, 16)
+    g.wait_ge(T.sem.st, 16 * len(mine))
+
+
+def rank_program(g, core, T, topo):
+    routes, calls = _plan(T, topo)
+    rank = T.rank_of(core)
+    if rank is None:
+        for r in routes:
+            if r["via"] == core:
+                _helper(g, core, T, topo, r)
+    elif rank in calls:
+        _rank_p(g, core, T, topo, calls[rank])
+    else:
+        _rank_q(g, core, T, topo, [r for r in routes if r["q"] == rank])

@@ -1,40 +1,26 @@
-from concourse.bass import DstId, RemoteDMATransfer
 from concourse.mybir import AluOpType
 
 TK = 128
-ON_CHIP = 8
-OFF_CHIP = 8
+NX = 512
 
 SCRATCH = {
-    "ws": ("sbuf", [128, 128], "bfloat16"),
-    "xs": ("sbuf", [128, 512], "bfloat16"),
-    "zs": ("sbuf", [128, 512], "float32"),
+    "xw": ("sbuf", [128, 640], "bfloat16"),
+    "rw": ("sbuf", [128, 256], "bfloat16"),
+    "zs": ("sbuf", [128, 128], "float32"),
     "hs": ("sbuf", [128, 512], "bfloat16"),
     "land": ("sbuf", [128, 512], "bfloat16"),
     "ys": ("sbuf", [128, 512], "bfloat16"),
     "ps0": ("psum", [128, 512], "float32"),
     "ps1": ("psum", [128, 512], "float32"),
     "ps2": ("psum", [128, 512], "float32"),
+    "ps3": ("psum", [128, 512], "float32"),
 }
-SEMAPHORES = ["ld", "zero", "mm0", "mm1", "mm2", "ev0", "ev1", "ev2", "relay", "arr0", "arr1", "arr2", "sent", "st"]
+SEMAPHORES = ["ld", "zero", "mm0", "mm1", "mm2", "mm3", "ev0", "ev1", "ev2", "ev3", "relay",
+              "arr0", "arr1", "arr2", "arr3", "sent", "st"]
 
 
-def _bits(mask):
-    return [b for b in range(mask.bit_length()) if (mask >> b) & 1]
-
-
-def _mask(bits):
-    m = 0
-    for b in bits:
-        m |= 1 << b
-    return m
-
-
-def _pow2(n):
-    k = 1
-    while 2 * k <= n:
-        k *= 2
-    return k
+def _count(mask):
+    return sum((mask >> b) & 1 for b in range(mask.bit_length()))
 
 
 def _plan(T, topo):
@@ -43,132 +29,145 @@ def _plan(T, topo):
     for p in range(len(dest)):
         byq = {}
         for c, q in enumerate(dest[p]):
-            if q not in byq:
-                byq[q] = {"p": p, "q": q, "blocks": [], "slot": nslot.get(q, 0), "via": None}
-            byq[q]["blocks"].append(c)
+            far = not topo.may_write(cores[p], cores[q])
+            raw = far and c == len(dest[p]) - 1
+            if raw or q not in byq:
+                r = {"p": p, "q": q, "blocks": [], "slot": nslot.get(q, 0), "via": None, "far": far, "raw": raw}
+                routes.append(r)
+                if not raw:
+                    byq[q] = r
+            else:
+                r = byq[q]
+            r["blocks"].append(c)
             nslot[q] = nslot.get(q, 0) + 1
-        routes.extend(byq[q] for q in sorted(byq))
+    early = [any(r["raw"] for r in routes if r["p"] == p) for p in range(len(dest))]
+
+    def free(src, dst):
+        return [c for c in range(topo.CORES_PER_CHIP * topo.CHIPS)
+                if topo.chip(c) == topo.chip(src) and c not in used and topo.may_write(c, dst)]
 
     out_load, in_load, used = {}, {}, set(cores)
-    for r in sorted(routes, key=lambda r: (-len(r["blocks"]), r["p"], r["q"])):
+    for r in sorted((r for r in routes if not r["far"]), key=lambda r: (early[r["p"]], r["p"], r["q"])):
         src, dst, n = cores[r["p"]], cores[r["q"]], len(r["blocks"])
-        if topo.may_write(src, dst):
-            continue
-        cands = [c for c in range(topo.CORES_PER_CHIP * topo.CHIPS)
-                 if topo.chip(c) == topo.chip(src) and c not in used and topo.may_write(c, dst)]
-        via = min(cands, key=lambda c: (max(out_load.get((topo.chip(src), topo.die(c)), 0),
-                                            in_load.get((topo.chip(dst), topo.die(c)), 0)),
-                                        topo.die(c) != topo.die(src), c))
+        port = (topo.chip(dst), topo.die(src))
+        cands = [c for c in free(src, dst) if topo.die(c) != topo.die(src)]
+        if cands:
+            via = min(cands, key=lambda c: (in_load.get((topo.chip(dst), topo.die(c)), 0), c))
+            if in_load.get(port, 0) >= in_load.get((topo.chip(dst), topo.die(via)), 0) + n:
+                port = (topo.chip(dst), topo.die(via))
+                used.add(via)
+                r["far"], r["via"], r["mask2"] = True, via, topo.mask(via, dst)
+        in_load[port] = in_load.get(port, 0) + n
+
+    for r in sorted((r for r in routes if r["far"] and r["via"] is None),
+                    key=lambda r: (-len(r["blocks"]), r["p"], r["q"], r["slot"])):
+        src, dst, n = cores[r["p"]], cores[r["q"]], len(r["blocks"])
+        via = min(free(src, dst), key=lambda c: (max(out_load.get((topo.chip(src), topo.die(c)), 0),
+                                                     in_load.get((topo.chip(dst), topo.die(c)), 0)),
+                                                 topo.die(c) != topo.die(src), c))
         d = topo.die(via)
         out_load[(topo.chip(src), d)] = out_load.get((topo.chip(src), d), 0) + n
         in_load[(topo.chip(dst), d)] = in_load.get((topo.chip(dst), d), 0) + n
         used.add(via)
         r["via"] = via
-        r["mask2"] = _mask(_bits(topo.mask(via, dst))[:OFF_CHIP])
+        r["mask2"] = topo.mask(via, dst)
 
-    calls = {}
+    order = {}
     for p in range(len(dest)):
-        mine = sorted((r for r in routes if r["p"] == p), key=lambda r: (r["via"] is None, len(r["blocks"]), r["q"]))
-        off, calls[p] = 0, []
-        for k, r in enumerate(mine):
+        order[p] = sorted((r for r in routes if r["p"] == p),
+                          key=lambda r: (0 if r["raw"] else 1 if r["far"] else 2, -len(r["blocks"]),
+                                         not r["far"] or topo.die(r["via"]) == topo.die(cores[p]), r["q"]))
+        off = 0
+        for k, r in enumerate(order[p]):
             r["k"], r["off"] = k, off
-            off += TK * len(r["blocks"])
-            r["hop"] = cores[r["q"]] if r["via"] is None else r["via"]
-            last = calls[p][-1] if calls[p] else None
-            if last and (last[0]["via"] is None) == (r["via"] is None) and len(last[0]["blocks"]) == len(r["blocks"]):
-                last.append(r)
-            else:
-                calls[p].append([r])
-        for call in calls[p]:
-            common = topo.mask(cores[p], call[0]["hop"])
-            for r in call:
-                common &= topo.mask(cores[p], r["hop"])
-            bits = _bits(common)
-            for j, r in enumerate(call):
-                cap = ON_CHIP if topo.chip(r["hop"]) == topo.chip(cores[p]) else OFF_CHIP
-                r["mask1"] = _mask(bits[j::len(call)][:min(cap, _pow2(len(bits) // len(call)))])
-    return routes, calls
+            if not r["raw"]:
+                off += TK * len(r["blocks"])
+            r["hop"] = r["via"] if r["far"] else cores[r["q"]]
+            r["mask1"] = topo.mask(cores[p], r["hop"])
+    return routes, order
 
 
-def _count(mask):
-    return len(_bits(mask))
-
-
-def _rank_p(g, core, T, topo, calls):
-    mine = [r for call in calls for r in call]
-    widest = TK * max(len(r["blocks"]) for r in mine)
-    g.sync.dma_start(T.ws[:, :], T.w[:, :]).then_inc(T.sem.ld, 16)
-    g.scalar.dma_start(T.xs[:, :], T.x[:, :]).then_inc(T.sem.ld, 16)
-    g.vector.memset(T.zs[:, 0:widest], 0.0).then_inc(T.sem.zero, 1)
+def _rank_p(g, core, T, topo, mine):
+    w = T.xw[:, NX:NX + TK]
+    g.sync.dma_start(w, T.w[:, :]).then_inc(T.sem.ld, 16)
+    g.scalar.dma_start(T.xw[:, 0:NX], T.x[:, :]).then_inc(T.sem.ld, 16)
+    g.vector.memset(T.zs[:, :], 0.0).then_inc(T.sem.zero, 1)
     g.vector.wait_ge(T.sem.zero, 1)
     g.tensor.wait_ge(T.sem.ld, 32)
+    left, b = 0, 0
     for r in mine:
-        ps, mm, ev = T["ps%d" % r["k"]], T.sem["mm%d" % r["k"]], T.sem["ev%d" % r["k"]]
-        runs = []
-        for c in r["blocks"]:
-            if runs and runs[-1][0] + runs[-1][1] == c:
-                runs[-1][1] += 1
-            else:
-                runs.append([c, 1])
-        col = 0
-        for c0, n in runs:
-            g.tensor.matmul(ps[:, col:col + n * TK], T.ws[:, :], T.xs[:, c0 * TK:(c0 + n) * TK], True, True).then_inc(mm, 1)
-            col += n * TK
-        g.vector.wait_ge(mm, len(runs))
-        g.vector.tensor_tensor(T.hs[:, r["off"]:r["off"] + col], ps[:, 0:col], T.zs[:, 0:col], AluOpType.max).then_inc(ev, 1)
-    left = 0
-    for call in calls:
-        transfers = []
-        for r in call:
-            g.wait_ge(T.sem["ev%d" % r["k"]], 1)
-            n = TK * len(r["blocks"])
-            rid, pid, _ = topo.addr(r["hop"])
-            if r["via"] is None:
-                out, sem = T.land[:, TK * r["slot"]:TK * r["slot"] + n], T.sem["arr%d" % r["p"]]
-            else:
-                out, sem = T.hs[:, 0:n], T.sem.relay
-            transfers.append(RemoteDMATransfer(dst_ids=[DstId(rid=rid, pnc=pid)], dma_engine_mask=r["mask1"],
-                                               remote_sem=sem, src=T.hs[:, r["off"]:r["off"] + n], dst=out))
+        ev, n = T.sem["ev%d" % r["k"]], TK * len(r["blocks"])
+        rid, pid, _ = topo.addr(r["hop"])
+        if r["raw"]:
+            g.wait_ge(T.sem.ld, 32)
+            g.remote_dma(out_ap=T.rw[:, :], in_ap=T.xw[:, NX - TK:NX + TK], remote_sem=T.sem.relay, local_sem=T.sem.sent,
+                         pid=pid, routing_id=rid, dma_engine_mask=r["mask1"])
             left += _count(r["mask1"])
-        g.remote_dma_fused(transfers, local_sem=T.sem.sent)
+            continue
+        for j, c in enumerate(r["blocks"]):
+            ps, mm, o = T["ps%d" % b], T.sem["mm%d" % b], r["off"] + TK * j
+            g.tensor.matmul(ps[:, 0:TK], w, T.xw[:, c * TK:(c + 1) * TK], True, True).then_inc(mm, 1)
+            g.vector.wait_ge(mm, 1)
+            g.vector.tensor_tensor(T.hs[:, o:o + TK], ps[:, 0:TK], T.zs[:, :], AluOpType.max).then_inc(ev, 1)
+            b += 1
+        if r["far"]:
+            out, sem = T.hs[:, 0:n], T.sem.relay
+        else:
+            out, sem = T.land[:, TK * r["slot"]:TK * r["slot"] + n], T.sem["arr%d" % r["slot"]]
+        g.wait_ge(ev, len(r["blocks"]))
+        g.remote_dma(out_ap=out, in_ap=T.hs[:, r["off"]:r["off"] + n], remote_sem=sem, local_sem=T.sem.sent,
+                     pid=pid, routing_id=rid, dma_engine_mask=r["mask1"])
+        left += _count(r["mask1"])
     g.wait_ge(T.sem.sent, left)
 
 
 def _helper(g, core, T, topo, r):
     n = TK * len(r["blocks"])
     rid, pid, _ = topo.addr(T.cores[r["q"]])
-    g.wait_ge(T.sem.relay, _count(r["mask1"]))
+    if r["raw"]:
+        g.vector.memset(T.zs[:, :], 0.0).then_inc(T.sem.zero, 1)
+        g.vector.wait_ge(T.sem.zero, 1)
+        g.tensor.wait_ge(T.sem.relay, _count(r["mask1"]))
+        g.tensor.matmul(T.ps0[:, 0:TK], T.rw[:, TK:2 * TK], T.rw[:, 0:TK], True, True).then_inc(T.sem.mm0, 1)
+        g.vector.wait_ge(T.sem.mm0, 1)
+        g.vector.tensor_tensor(T.hs[:, 0:TK], T.ps0[:, 0:TK], T.zs[:, :], AluOpType.max).then_inc(T.sem.ev0, 1)
+        g.wait_ge(T.sem.ev0, 1)
+    else:
+        g.wait_ge(T.sem.relay, _count(r["mask1"]))
     g.remote_dma(out_ap=T.land[:, TK * r["slot"]:TK * r["slot"] + n], in_ap=T.hs[:, 0:n],
-                 remote_sem=T.sem["arr%d" % r["p"]], local_sem=T.sem.sent, pid=pid, routing_id=rid,
+                 remote_sem=T.sem["arr%d" % r["slot"]], local_sem=T.sem.sent, pid=pid, routing_id=rid,
                  dma_engine_mask=r["mask2"])
     g.wait_ge(T.sem.sent, _count(r["mask2"]))
 
 
 def _rank_q(g, core, T, topo, mine):
-    g.sync.dma_start(T.ws[:, :], T.w[:, :]).then_inc(T.sem.ld, 16)
+    w = T.xw[:, NX:NX + TK]
+    g.sync.dma_start(w, T.w[:, :]).then_inc(T.sem.ld, 16)
     g.tensor.wait_ge(T.sem.ld, 16)
-    mine = sorted(mine, key=lambda r: (len(r["blocks"]), r["p"]))
+    mine = sorted(mine, key=lambda r: (r["far"], r["k"], len(r["blocks"]), r["p"]))
     queues = [g.scalar, g.sync]
     for k, r in enumerate(mine):
         a, n = TK * r["slot"], TK * len(r["blocks"])
-        ps, mm, ev, dq = T["ps%d" % k], T.sem["mm%d" % k], T.sem["ev%d" % k], queues[k % 2]
-        g.tensor.wait_ge(T.sem["arr%d" % r["p"]], _count(r["mask1"] if r["via"] is None else r["mask2"]))
-        g.tensor.matmul(ps[:, 0:n], T.ws[:, :], T.land[:, a:a + n], True, True).then_inc(mm, 1)
-        g.vector.wait_ge(mm, 1)
-        g.vector.tensor_copy(T.ys[:, a:a + n], ps[:, 0:n]).then_inc(ev, 1)
-        dq.wait_ge(ev, 1)
+        ev, dq = T.sem["ev%d" % k], queues[k % 2]
+        g.tensor.wait_ge(T.sem["arr%d" % r["slot"]], _count(r["mask2"] if r["far"] else r["mask1"]))
+        for s in range(r["slot"], r["slot"] + len(r["blocks"])):
+            ps, mm = T["ps%d" % s], T.sem["mm%d" % s]
+            g.tensor.matmul(ps[:, 0:TK], w, T.land[:, TK * s:TK * s + TK], True, True).then_inc(mm, 1)
+            g.vector.wait_ge(mm, 1)
+            g.vector.tensor_copy(T.ys[:, TK * s:TK * s + TK], ps[:, 0:TK]).then_inc(ev, 1)
+        dq.wait_ge(ev, len(r["blocks"]))
         dq.dma_start(T.y[:, a:a + n], T.ys[:, a:a + n]).then_inc(T.sem.st, 16)
     g.wait_ge(T.sem.st, 16 * len(mine))
 
 
 def rank_program(g, core, T, topo):
-    routes, calls = _plan(T, topo)
+    routes, order = _plan(T, topo)
     rank = T.rank_of(core)
     if rank is None:
         for r in routes:
             if r["via"] == core:
                 _helper(g, core, T, topo, r)
-    elif rank in calls:
-        _rank_p(g, core, T, topo, calls[rank])
+    elif rank in order:
+        _rank_p(g, core, T, topo, order[rank])
     else:
         _rank_q(g, core, T, topo, [r for r in routes if r["q"] == rank])

@@ -1,12 +1,15 @@
 from concourse.mybir import AluOpType
 
 TK = 128
-NX = 512
+HK = 64
 
 SCRATCH = {
-    "xw": ("sbuf", [128, 640], "bfloat16"),
-    "rw": ("sbuf", [128, 256], "bfloat16"),
-    "zs": ("sbuf", [128, 128], "float32"),
+    "wd": ("dram", [128, 128], "bfloat16"),
+    "xs": ("sbuf", [128, 512], "bfloat16"),
+    "ws": ("sbuf", [128, 128], "bfloat16"),
+    "rw": ("sbuf", [128, 128], "bfloat16"),
+    "rx": ("sbuf", [128, 512], "bfloat16"),
+    "zs": ("sbuf", [128, 64], "float32"),
     "hs": ("sbuf", [128, 512], "bfloat16"),
     "land": ("sbuf", [128, 512], "bfloat16"),
     "ys": ("sbuf", [128, 512], "bfloat16"),
@@ -14,9 +17,13 @@ SCRATCH = {
     "ps1": ("psum", [128, 512], "float32"),
     "ps2": ("psum", [128, 512], "float32"),
     "ps3": ("psum", [128, 512], "float32"),
+    "ps4": ("psum", [128, 512], "float32"),
+    "ps5": ("psum", [128, 512], "float32"),
+    "ps6": ("psum", [128, 512], "float32"),
+    "ps7": ("psum", [128, 512], "float32"),
 }
-SEMAPHORES = ["ld", "zero", "mm0", "mm1", "mm2", "mm3", "ev0", "ev1", "ev2", "ev3", "relay",
-              "arr0", "arr1", "arr2", "arr3", "sent", "st"]
+SEMAPHORES = ["ldd", "ldx", "ldw", "zero", "mm0", "mm1", "mm2", "mm3", "mm4", "mm5", "mm6", "mm7",
+              "ev0", "ev1", "ev2", "ev3", "relay", "arr0", "arr1", "arr2", "arr3", "sent", "st"]
 
 
 def _count(mask):
@@ -29,38 +36,36 @@ def _plan(T, topo):
     for p in range(len(dest)):
         byq = {}
         for c, q in enumerate(dest[p]):
-            far = not topo.may_write(cores[p], cores[q])
-            raw = far and c == len(dest[p]) - 1
-            if raw or q not in byq:
-                r = {"p": p, "q": q, "blocks": [], "slot": nslot.get(q, 0), "via": None, "far": far, "raw": raw}
-                routes.append(r)
-                if not raw:
-                    byq[q] = r
-            else:
-                r = byq[q]
-            r["blocks"].append(c)
+            if q not in byq:
+                byq[q] = {"p": p, "q": q, "blocks": [], "slot": nslot.get(q, 0), "via": None, "raw": False,
+                          "far": not topo.may_write(cores[p], cores[q])}
+                routes.append(byq[q])
+            byq[q]["blocks"].append(c)
             nslot[q] = nslot.get(q, 0) + 1
-    early = [any(r["raw"] for r in routes if r["p"] == p) for p in range(len(dest))]
+    for r in routes:
+        r["waste"] = r["blocks"][-1] + 1 - r["blocks"][0] - len(r["blocks"])
+    used = set(cores)
 
     def free(src, dst):
         return [c for c in range(topo.CORES_PER_CHIP * topo.CHIPS)
                 if topo.chip(c) == topo.chip(src) and c not in used and topo.may_write(c, dst)]
 
-    out_load, in_load, used = {}, {}, set(cores)
-    for r in sorted((r for r in routes if not r["far"]), key=lambda r: (early[r["p"]], r["p"], r["q"])):
+    out_load, in_load = {}, {}
+    for r in sorted((r for r in routes if not r["far"]), key=lambda r: (-r["waste"], r["p"], r["q"])):
         src, dst, n = cores[r["p"]], cores[r["q"]], len(r["blocks"])
         port = (topo.chip(dst), topo.die(src))
         cands = [c for c in free(src, dst) if topo.die(c) != topo.die(src)]
         if cands:
-            via = min(cands, key=lambda c: (in_load.get((topo.chip(dst), topo.die(c)), 0), c))
+            via = min(cands, key=lambda c: (in_load.get((topo.chip(dst), topo.die(c)), 0),
+                                            any(topo.may_write(c, d) != topo.may_write(src, d) for d in cores), c))
             if in_load.get(port, 0) >= in_load.get((topo.chip(dst), topo.die(via)), 0) + n:
                 port = (topo.chip(dst), topo.die(via))
                 used.add(via)
-                r["far"], r["via"], r["mask2"] = True, via, topo.mask(via, dst)
+                r["far"], r["via"] = True, via
         in_load[port] = in_load.get(port, 0) + n
 
     for r in sorted((r for r in routes if r["far"] and r["via"] is None),
-                    key=lambda r: (-len(r["blocks"]), r["p"], r["q"], r["slot"])):
+                    key=lambda r: (-len(r["blocks"]), r["p"], r["q"])):
         src, dst, n = cores[r["p"]], cores[r["q"]], len(r["blocks"])
         via = min(free(src, dst), key=lambda c: (max(out_load.get((topo.chip(src), topo.die(c)), 0),
                                                      in_load.get((topo.chip(dst), topo.die(c)), 0)),
@@ -70,10 +75,13 @@ def _plan(T, topo):
         in_load[(topo.chip(dst), d)] = in_load.get((topo.chip(dst), d), 0) + n
         used.add(via)
         r["via"] = via
-        r["mask2"] = topo.mask(via, dst)
 
     order = {}
     for p in range(len(dest)):
+        far = [r for r in routes if r["p"] == p and r["far"]]
+        if far:
+            min(far, key=lambda r: (-len(r["blocks"]), r["waste"], topo.die(r["via"]) != topo.die(cores[p]),
+                                    -r["blocks"][0]))["raw"] = True
         order[p] = sorted((r for r in routes if r["p"] == p),
                           key=lambda r: (0 if r["raw"] else 1 if r["far"] else 2, -len(r["blocks"]),
                                          not r["far"] or topo.die(r["via"]) == topo.die(cores[p]), r["q"]))
@@ -84,37 +92,59 @@ def _plan(T, topo):
                 off += TK * len(r["blocks"])
             r["hop"] = r["via"] if r["far"] else cores[r["q"]]
             r["mask1"] = topo.mask(cores[p], r["hop"])
+            if r["far"]:
+                r["mask2"] = topo.mask(r["via"], cores[r["q"]])
     return routes, order
 
 
-def _rank_p(g, core, T, topo, mine):
-    w = T.xw[:, NX:NX + TK]
-    g.sync.dma_start(w, T.w[:, :]).then_inc(T.sem.ld, 16)
-    g.scalar.dma_start(T.xw[:, 0:NX], T.x[:, :]).then_inc(T.sem.ld, 16)
+def _block(g, T, bank, w, src, a, dst, o, ev, clamp):
+    for h in range(0, TK, HK):
+        ps, mm = T["ps%d" % bank[0]], T.sem["mm%d" % bank[0]]
+        bank[0] += 1
+        g.tensor.matmul(ps[:, 0:HK], w, src[:, a + h:a + h + HK], True, True).then_inc(mm, 1)
+        g.vector.wait_ge(mm, 1)
+        if clamp:
+            g.vector.tensor_tensor(dst[:, o + h:o + h + HK], ps[:, 0:HK], T.zs[:, :], AluOpType.max).then_inc(ev, 1)
+        else:
+            g.vector.tensor_copy(dst[:, o + h:o + h + HK], ps[:, 0:HK]).then_inc(ev, 1)
+    return TK // HK
+
+
+def _zeros(g, T):
     g.vector.memset(T.zs[:, :], 0.0).then_inc(T.sem.zero, 1)
     g.vector.wait_ge(T.sem.zero, 1)
-    g.tensor.wait_ge(T.sem.ld, 32)
-    left, b = 0, 0
+
+
+def _rank_p(g, core, T, topo, mine):
+    if mine[0]["raw"]:
+        g.sync.dma_start(T.wd[:, :], T.w[:, :]).then_inc(T.sem.ldd, 16)
+    g.scalar.dma_start(T.xs[:, :], T.x[:, :]).then_inc(T.sem.ldx, 16)
+    g.sync.dma_start(T.ws[:, :], T.w[:, :]).then_inc(T.sem.ldw, 16)
+    _zeros(g, T)
+    g.tensor.wait_ge(T.sem.ldx, 16)
+    g.tensor.wait_ge(T.sem.ldw, 16)
+    left, bank = 0, [0]
     for r in mine:
         ev, n = T.sem["ev%d" % r["k"]], TK * len(r["blocks"])
         rid, pid, _ = topo.addr(r["hop"])
         if r["raw"]:
-            g.wait_ge(T.sem.ld, 32)
-            g.remote_dma(out_ap=T.rw[:, :], in_ap=T.xw[:, NX - TK:NX + TK], remote_sem=T.sem.relay, local_sem=T.sem.sent,
+            lo, hi = TK * r["blocks"][0], TK * (r["blocks"][-1] + 1)
+            g.wait_ge(T.sem.ldd, 16)
+            g.remote_dma(out_ap=T.rw[:, :], in_ap=T.wd[:, :], remote_sem=T.sem.relay, local_sem=T.sem.sent,
                          pid=pid, routing_id=rid, dma_engine_mask=r["mask1"])
-            left += _count(r["mask1"])
+            g.wait_ge(T.sem.ldx, 16)
+            g.remote_dma(out_ap=T.rx[:, 0:hi - lo], in_ap=T.xs[:, lo:hi], remote_sem=T.sem.relay, local_sem=T.sem.sent,
+                         pid=pid, routing_id=rid, dma_engine_mask=r["mask1"])
+            left += 2 * _count(r["mask1"])
             continue
+        done = 0
         for j, c in enumerate(r["blocks"]):
-            ps, mm, o = T["ps%d" % b], T.sem["mm%d" % b], r["off"] + TK * j
-            g.tensor.matmul(ps[:, 0:TK], w, T.xw[:, c * TK:(c + 1) * TK], True, True).then_inc(mm, 1)
-            g.vector.wait_ge(mm, 1)
-            g.vector.tensor_tensor(T.hs[:, o:o + TK], ps[:, 0:TK], T.zs[:, :], AluOpType.max).then_inc(ev, 1)
-            b += 1
+            done += _block(g, T, bank, T.ws[:, :], T.xs, TK * c, T.hs, r["off"] + TK * j, ev, True)
         if r["far"]:
             out, sem = T.hs[:, 0:n], T.sem.relay
         else:
             out, sem = T.land[:, TK * r["slot"]:TK * r["slot"] + n], T.sem["arr%d" % r["slot"]]
-        g.wait_ge(ev, len(r["blocks"]))
+        g.wait_ge(ev, done)
         g.remote_dma(out_ap=out, in_ap=T.hs[:, r["off"]:r["off"] + n], remote_sem=sem, local_sem=T.sem.sent,
                      pid=pid, routing_id=rid, dma_engine_mask=r["mask1"])
         left += _count(r["mask1"])
@@ -125,13 +155,12 @@ def _helper(g, core, T, topo, r):
     n = TK * len(r["blocks"])
     rid, pid, _ = topo.addr(T.cores[r["q"]])
     if r["raw"]:
-        g.vector.memset(T.zs[:, :], 0.0).then_inc(T.sem.zero, 1)
-        g.vector.wait_ge(T.sem.zero, 1)
-        g.tensor.wait_ge(T.sem.relay, _count(r["mask1"]))
-        g.tensor.matmul(T.ps0[:, 0:TK], T.rw[:, TK:2 * TK], T.rw[:, 0:TK], True, True).then_inc(T.sem.mm0, 1)
-        g.vector.wait_ge(T.sem.mm0, 1)
-        g.vector.tensor_tensor(T.hs[:, 0:TK], T.ps0[:, 0:TK], T.zs[:, :], AluOpType.max).then_inc(T.sem.ev0, 1)
-        g.wait_ge(T.sem.ev0, 1)
+        _zeros(g, T)
+        g.tensor.wait_ge(T.sem.relay, 2 * _count(r["mask1"]))
+        done, bank = 0, [0]
+        for j, c in enumerate(r["blocks"]):
+            done += _block(g, T, bank, T.rw[:, :], T.rx, TK * (c - r["blocks"][0]), T.hs, TK * j, T.sem.ev0, True)
+        g.wait_ge(T.sem.ev0, done)
     else:
         g.wait_ge(T.sem.relay, _count(r["mask1"]))
     g.remote_dma(out_ap=T.land[:, TK * r["slot"]:TK * r["slot"] + n], in_ap=T.hs[:, 0:n],
@@ -141,21 +170,17 @@ def _helper(g, core, T, topo, r):
 
 
 def _rank_q(g, core, T, topo, mine):
-    w = T.xw[:, NX:NX + TK]
-    g.sync.dma_start(w, T.w[:, :]).then_inc(T.sem.ld, 16)
-    g.tensor.wait_ge(T.sem.ld, 16)
-    mine = sorted(mine, key=lambda r: (r["far"], r["k"], len(r["blocks"]), r["p"]))
-    queues = [g.scalar, g.sync]
+    g.sync.dma_start(T.ws[:, :], T.w[:, :]).then_inc(T.sem.ldw, 16)
+    g.tensor.wait_ge(T.sem.ldw, 16)
+    mine = sorted(mine, key=lambda r: (r["far"], len(r["blocks"]), r["k"], r["p"]))
+    queues, bank = [g.scalar, g.sync], [0]
     for k, r in enumerate(mine):
         a, n = TK * r["slot"], TK * len(r["blocks"])
-        ev, dq = T.sem["ev%d" % k], queues[k % 2]
+        ev, dq, done = T.sem["ev%d" % k], queues[k % 2], 0
         g.tensor.wait_ge(T.sem["arr%d" % r["slot"]], _count(r["mask2"] if r["far"] else r["mask1"]))
         for s in range(r["slot"], r["slot"] + len(r["blocks"])):
-            ps, mm = T["ps%d" % s], T.sem["mm%d" % s]
-            g.tensor.matmul(ps[:, 0:TK], w, T.land[:, TK * s:TK * s + TK], True, True).then_inc(mm, 1)
-            g.vector.wait_ge(mm, 1)
-            g.vector.tensor_copy(T.ys[:, TK * s:TK * s + TK], ps[:, 0:TK]).then_inc(ev, 1)
-        dq.wait_ge(ev, len(r["blocks"]))
+            done += _block(g, T, bank, T.ws[:, :], T.land, TK * s, T.ys, TK * s, ev, False)
+        dq.wait_ge(ev, done)
         dq.dma_start(T.y[:, a:a + n], T.ys[:, a:a + n]).then_inc(T.sem.st, 16)
     g.wait_ge(T.sem.st, 16 * len(mine))
 

from concourse.mybir import AluOpType

TK = 128
HK = 64

SCRATCH = {
    "wd": ("dram", [128, 128], "bfloat16"),
    "xs": ("sbuf", [128, 512], "bfloat16"),
    "ws": ("sbuf", [128, 128], "bfloat16"),
    "rw": ("sbuf", [128, 128], "bfloat16"),
    "rx": ("sbuf", [128, 512], "bfloat16"),
    "zs": ("sbuf", [128, 64], "float32"),
    "hs": ("sbuf", [128, 512], "bfloat16"),
    "land": ("sbuf", [128, 512], "bfloat16"),
    "ys": ("sbuf", [128, 512], "bfloat16"),
    "ps0": ("psum", [128, 512], "float32"),
    "ps1": ("psum", [128, 512], "float32"),
    "ps2": ("psum", [128, 512], "float32"),
    "ps3": ("psum", [128, 512], "float32"),
    "ps4": ("psum", [128, 512], "float32"),
    "ps5": ("psum", [128, 512], "float32"),
    "ps6": ("psum", [128, 512], "float32"),
    "ps7": ("psum", [128, 512], "float32"),
}
SEMAPHORES = ["ldd", "ldx", "ldw", "zero", "mm0", "mm1", "mm2", "mm3", "mm4", "mm5", "mm6", "mm7",
              "ev0", "ev1", "ev2", "ev3", "relay", "arr0", "arr1", "arr2", "arr3", "sent", "st"]


def _count(mask):
    return sum((mask >> b) & 1 for b in range(mask.bit_length()))


def _plan(T, topo):
    dest, cores = T.tables["DEST"], list(T.cores)
    routes, nslot = [], {}
    for p in range(len(dest)):
        byq = {}
        for c, q in enumerate(dest[p]):
            if q not in byq:
                byq[q] = {"p": p, "q": q, "blocks": [], "slot": nslot.get(q, 0), "via": None, "raw": False,
                          "far": not topo.may_write(cores[p], cores[q])}
                routes.append(byq[q])
            byq[q]["blocks"].append(c)
            nslot[q] = nslot.get(q, 0) + 1
    for r in routes:
        r["waste"] = r["blocks"][-1] + 1 - r["blocks"][0] - len(r["blocks"])
    used = set(cores)

    def free(src, dst):
        return [c for c in range(topo.CORES_PER_CHIP * topo.CHIPS)
                if topo.chip(c) == topo.chip(src) and c not in used and topo.may_write(c, dst)]

    out_load, in_load = {}, {}
    for r in sorted((r for r in routes if not r["far"]), key=lambda r: (-r["waste"], r["p"], r["q"])):
        src, dst, n = cores[r["p"]], cores[r["q"]], len(r["blocks"])
        port = (topo.chip(dst), topo.die(src))
        cands = [c for c in free(src, dst) if topo.die(c) != topo.die(src)]
        if cands:
            via = min(cands, key=lambda c: (in_load.get((topo.chip(dst), topo.die(c)), 0),
                                            any(topo.may_write(c, d) != topo.may_write(src, d) for d in cores), c))
            if in_load.get(port, 0) >= in_load.get((topo.chip(dst), topo.die(via)), 0) + n:
                port = (topo.chip(dst), topo.die(via))
                used.add(via)
                r["far"], r["via"] = True, via
        in_load[port] = in_load.get(port, 0) + n

    for r in sorted((r for r in routes if r["far"] and r["via"] is None),
                    key=lambda r: (-len(r["blocks"]), r["p"], r["q"])):
        src, dst, n = cores[r["p"]], cores[r["q"]], len(r["blocks"])
        via = min(free(src, dst), key=lambda c: (max(out_load.get((topo.chip(src), topo.die(c)), 0),
                                                     in_load.get((topo.chip(dst), topo.die(c)), 0)),
                                                 topo.die(c) != topo.die(src), c))
        d = topo.die(via)
        out_load[(topo.chip(src), d)] = out_load.get((topo.chip(src), d), 0) + n
        in_load[(topo.chip(dst), d)] = in_load.get((topo.chip(dst), d), 0) + n
        used.add(via)
        r["via"] = via

    order = {}
    for p in range(len(dest)):
        far = [r for r in routes if r["p"] == p and r["far"]]
        if far:
            min(far, key=lambda r: (-len(r["blocks"]), r["waste"], topo.die(r["via"]) != topo.die(cores[p]),
                                    -r["blocks"][0]))["raw"] = True
        order[p] = sorted((r for r in routes if r["p"] == p),
                          key=lambda r: (0 if r["raw"] else 1 if r["far"] else 2, -len(r["blocks"]),
                                         not r["far"] or topo.die(r["via"]) == topo.die(cores[p]), r["q"]))
        off = 0
        for k, r in enumerate(order[p]):
            r["k"], r["off"] = k, off
            if not r["raw"]:
                off += TK * len(r["blocks"])
            r["hop"] = r["via"] if r["far"] else cores[r["q"]]
            r["mask1"] = topo.mask(cores[p], r["hop"])
            if r["far"]:
                r["mask2"] = topo.mask(r["via"], cores[r["q"]])
    return routes, order


def _block(g, T, bank, w, src, a, dst, o, ev, clamp):
    for h in range(0, TK, HK):
        ps, mm = T["ps%d" % bank[0]], T.sem["mm%d" % bank[0]]
        bank[0] += 1
        g.tensor.matmul(ps[:, 0:HK], w, src[:, a + h:a + h + HK], True, True).then_inc(mm, 1)
        g.vector.wait_ge(mm, 1)
        if clamp:
            g.vector.tensor_tensor(dst[:, o + h:o + h + HK], ps[:, 0:HK], T.zs[:, :], AluOpType.max).then_inc(ev, 1)
        else:
            g.vector.tensor_copy(dst[:, o + h:o + h + HK], ps[:, 0:HK]).then_inc(ev, 1)
    return TK // HK


def _zeros(g, T):
    g.vector.memset(T.zs[:, :], 0.0).then_inc(T.sem.zero, 1)
    g.vector.wait_ge(T.sem.zero, 1)


def _rank_p(g, core, T, topo, mine):
    if mine[0]["raw"]:
        g.sync.dma_start(T.wd[:, :], T.w[:, :]).then_inc(T.sem.ldd, 16)
    g.scalar.dma_start(T.xs[:, :], T.x[:, :]).then_inc(T.sem.ldx, 16)
    g.sync.dma_start(T.ws[:, :], T.w[:, :]).then_inc(T.sem.ldw, 16)
    _zeros(g, T)
    g.tensor.wait_ge(T.sem.ldx, 16)
    g.tensor.wait_ge(T.sem.ldw, 16)
    left, bank = 0, [0]
    for r in mine:
        ev, n = T.sem["ev%d" % r["k"]], TK * len(r["blocks"])
        rid, pid, _ = topo.addr(r["hop"])
        if r["raw"]:
            lo, hi = TK * r["blocks"][0], TK * (r["blocks"][-1] + 1)
            g.wait_ge(T.sem.ldd, 16)
            g.remote_dma(out_ap=T.rw[:, :], in_ap=T.wd[:, :], remote_sem=T.sem.relay, local_sem=T.sem.sent,
                         pid=pid, routing_id=rid, dma_engine_mask=r["mask1"])
            g.wait_ge(T.sem.ldx, 16)
            g.remote_dma(out_ap=T.rx[:, 0:hi - lo], in_ap=T.xs[:, lo:hi], remote_sem=T.sem.relay, local_sem=T.sem.sent,
                         pid=pid, routing_id=rid, dma_engine_mask=r["mask1"])
            left += 2 * _count(r["mask1"])
            continue
        done = 0
        for j, c in enumerate(r["blocks"]):
            done += _block(g, T, bank, T.ws[:, :], T.xs, TK * c, T.hs, r["off"] + TK * j, ev, True)
        if r["far"]:
            out, sem = T.hs[:, 0:n], T.sem.relay
        else:
            out, sem = T.land[:, TK * r["slot"]:TK * r["slot"] + n], T.sem["arr%d" % r["slot"]]
        g.wait_ge(ev, done)
        g.remote_dma(out_ap=out, in_ap=T.hs[:, r["off"]:r["off"] + n], remote_sem=sem, local_sem=T.sem.sent,
                     pid=pid, routing_id=rid, dma_engine_mask=r["mask1"])
        left += _count(r["mask1"])
    g.wait_ge(T.sem.sent, left)


def _helper(g, core, T, topo, r):
    n = TK * len(r["blocks"])
    rid, pid, _ = topo.addr(T.cores[r["q"]])
    if r["raw"]:
        _zeros(g, T)
        g.tensor.wait_ge(T.sem.relay, 2 * _count(r["mask1"]))
        done, bank = 0, [0]
        for j, c in enumerate(r["blocks"]):
            done += _block(g, T, bank, T.rw[:, :], T.rx, TK * (c - r["blocks"][0]), T.hs, TK * j, T.sem.ev0, True)
        g.wait_ge(T.sem.ev0, done)
    else:
        g.wait_ge(T.sem.relay, _count(r["mask1"]))
    g.remote_dma(out_ap=T.land[:, TK * r["slot"]:TK * r["slot"] + n], in_ap=T.hs[:, 0:n],
                 remote_sem=T.sem["arr%d" % r["slot"]], local_sem=T.sem.sent, pid=pid, routing_id=rid,
                 dma_engine_mask=r["mask2"])
    g.wait_ge(T.sem.sent, _count(r["mask2"]))


def _rank_q(g, core, T, topo, mine):
    g.sync.dma_start(T.ws[:, :], T.w[:, :]).then_inc(T.sem.ldw, 16)
    g.tensor.wait_ge(T.sem.ldw, 16)
    mine = sorted(mine, key=lambda r: (r["far"], len(r["blocks"]), r["k"], r["p"]))
    queues, bank = [g.scalar, g.sync], [0]
    for k, r in enumerate(mine):
        a, n = TK * r["slot"], TK * len(r["blocks"])
        ev, dq, done = T.sem["ev%d" % k], queues[k % 2], 0
        g.tensor.wait_ge(T.sem["arr%d" % r["slot"]], _count(r["mask2"] if r["far"] else r["mask1"]))
        for s in range(r["slot"], r["slot"] + len(r["blocks"])):
            done += _block(g, T, bank, T.ws[:, :], T.land, TK * s, T.ys, TK * s, ev, False)
        dq.wait_ge(ev, done)
        dq.dma_start(T.y[:, a:a + n], T.ys[:, a:a + n]).then_inc(T.sem.st, 16)
    g.wait_ge(T.sem.st, 16 * len(mine))


def rank_program(g, core, T, topo):
    routes, order = _plan(T, topo)
    rank = T.rank_of(core)
    if rank is None:
        for r in routes:
            if r["via"] == core:
                _helper(g, core, T, topo, r)
    elif rank in order:
        _rank_p(g, core, T, topo, order[rank])
    else:
        _rank_q(g, core, T, topo, [r for r in routes if r["q"] == rank])
